import numpy as np, ml_dtypes
CORES = [16,17,18,19,32,33,34,35]
N = 8
BF = ml_dtypes.bfloat16
def entries(a):
    return np.ascontiguousarray(a.T).reshape(-1)
def table(e):
    return np.ascontiguousarray(np.reshape(e, (-1, 16)).T).astype(np.int32)
def f(rng, *shape):
    return (rng.standard_normal(shape, dtype=np.float32) * np.exp2(rng.integers(-2, 3, shape[:-1] + (1,)))).astype(BF)
def wide(rng, *shape):
    v = f(rng, *shape).astype(np.float32); k = shape[:-2] + (1, shape[-1])
    return (v * np.exp2(rng.integers(-6, 7, k)) * (rng.random(k) > 0.0625)).astype(BF)
R, S1, S2, CAPP = 3072, 1024, 768, 16
T1, T2 = 0, 100
def orders(rng):
    return np.stack([rng.permutation(R) for r in range(N)])
def values(rng, order, n1, m, lo):
    v = rng.integers(-60, 1, (N, R))
    for r in range(N):
        v[r, order[r, :n1[r]]] = rng.integers(1, 5, n1[r]); v[r, order[r, :m[r]]] = rng.integers(lo[r], 256, m[r])
    x = f(rng, N, 16, R); x[:, 0] = v.astype(np.float32).astype(BF); return x
def some(rng, order, n1, m, *shape):
    top = np.array([m, n1, R])[rng.integers(0, 3, shape)]
    return order[(rng.random(shape) * top).astype(np.int64)]
def ghosts(rng, r, *shape):
    return R + ((r + 1 + rng.integers(0, N - 1, shape)) % N) * CAPP + rng.integers(0, CAPP, shape)
def draw(rng, order, n1, m, lo):
    x = values(rng, order, n1, m, lo); nb = []; bd = []
    for r in range(N):
        nb.append(np.where(rng.random((6, R)) < 0.7, some(rng, order[r], n1[r], m[r], 6, R), ghosts(rng, r, 6, R)))
        bd.append(table(some(rng, order[r], n1[r], m[r], N * CAPP)))
    return {"x": x, "nb": np.stack(nb).astype(np.int32), "bd": np.stack(bd)}
def setup_inputs(rng):
    return draw(rng, orders(rng), rng.integers(3 * S1 // 4, S1 + 1, N), np.full(N, S2 // 8), np.full(N, 40))
def setup_inputs_full(rng):
    order = orders(rng); a = int(rng.integers(0, N)); order[a] = np.arange(R); order[(a + 1) % N] = np.arange(R)[::-1]
    return draw(rng, order, np.full(N, S1), np.full(N, S2 // 8), np.full(N, 200))
def setup_inputs_ties(rng):
    order = orders(rng); n1 = rng.integers(3 * S1 // 4, S1 + 1, N); m = S2 // 8
    d = draw(rng, order, n1, np.full(N, m), np.full(N, 40)); x, nb = d["x"], d["nb"]; bd = []
    for r in range(N):
        h = order[r, :m]; c = order[r, n1[r]:]
        x[r, 0, h] = rng.integers(99, 102, m).astype(np.float32).astype(BF); x[r, 0, c] = rng.integers(-1, 1, len(c)).astype(np.float32).astype(BF)
        nb[r][:, h] = np.where(rng.random((6, m)) < 0.5, h[rng.integers(0, m, (6, m))], ghosts(rng, r, 6, m))
        nb[r][:, h[0]] = h[0]; x[r, 0, h[0]] = 100; nb[r][:, h[1]] = h[1]; x[r, 0, h[1]] = 101
        bd.append(table(h[rng.integers(0, m, N * CAPP)]))
    d["bd"] = np.stack(bd); return d
def setup_inputs_thin(rng):
    order = orders(rng); n1 = rng.integers(3 * S1 // 4, S1 + 1, N); m = np.minimum(S2 // 4, n1)
    d = draw(rng, order, n1, m, np.full(N, 40)); x, nb, bd = d["x"], d["nb"], d["bd"]; first = int(rng.integers(0, 6))
    for r in range(N):
        k = int(m[r]); h = order[r, :k]; c = order[r, n1[r]:]
        x[r, 0, h] = rng.integers(101, 104, k).astype(np.float32).astype(BF)
        nb[r][:, h] = np.where(rng.random((6, k)) < 0.5, h[rng.integers(0, k, (6, k))], ghosts(rng, r, 6, k))
        nb[r][(first + r) % 6, h] = c[rng.integers(0, len(c), k)]
        bd[r] = table(h[rng.integers(0, k, N * CAPP)])
    return d
def setup_inputs_far(rng):
    order = orders(rng); n1 = rng.integers(3 * S1 // 4, S1 + 1, N); m = np.full(N, S2 // 8); lo = np.full(N, 40); a = int(rng.integers(0, N)); b = (a + 1) % N; s = int(rng.integers(1, N))
    n1[a] = S1 // 8; m[a] = S2 // 64; lo[a] = 200
    d = draw(rng, order, n1, m, lo); nb, bd = d["nb"], d["bd"]
    for r in range(N):
        if r != a: nb[r] = R + ((r + s) % N) * CAPP + rng.integers(0, CAPP, (6, R))
        top = np.where(rng.random(N * CAPP) < 0.5, m[r], n1[r]); e = (rng.random(N * CAPP) * top).astype(np.int64)
        if r == a: e = rng.integers(n1[a], R, N * CAPP)
        if r == b: e = rng.integers(0, m[b], N * CAPP)
        bd[r] = table(order[r][e])
    return d
def setup_inputs_spread(rng):
    d = setup_inputs(rng); d["x"][:, 1:] = wide(rng, N, 16, R)[:, 1:]; return d
def grow(x, nb, bd):
    v = np.concatenate([a.astype(np.float64).T for a in x])
    w = np.stack([entries(a) for a in bd]).astype(np.int64).reshape(N, N, CAPP); near = []
    for r in range(N):
        ext = np.concatenate([r * R + np.arange(R), (R * np.arange(N)[:, None] + w[:, r]).reshape(-1)])
        near.append(ext[nb[r]].T)
    near = np.concatenate(near)
    p = np.flatnonzero(v[:, 0] > T1); number = np.full(N * R, -1); number[p] = np.arange(len(p)); kids = []
    for o in range(8):
        c = v[p].copy()
        for d in range(3): c += 0.125 * (v[near[p, 2 * d + (o >> d & 1)]] - v[p])
        kids.append(c)
    return v, near, p, number, np.stack(kids)
def check_inputs(d):
    bad = []; x = d["x"].astype(np.float32); nb, bd = d["nb"], d["bd"]
    if not np.isfinite(x).all() or not (np.abs(x) <= 65536).all(): bad.append("x finite and of size at most 65536")
    elif (x[:, 0] != np.floor(x[:, 0])).any() or (np.abs(x[:, 0]) > 256).any(): bad.append("x channel 0")
    own = (nb - R) // CAPP == np.arange(N)[:, None, None]
    if (nb < 0).any() or (nb >= R + N * CAPP).any() or own.any(): bad.append("nb")
    if (bd < 0).any() or (bd >= R).any(): bad.append("bd")
    if bad: return bad
    v, near, p, number, c1 = grow(d["x"], nb, bd); q = p // R
    if (np.bincount(q, minlength=N) > S1).any(): bad.append("splits of level 1")
    if (np.bincount(q[np.nonzero(c1[:, :, 0] > T2)[1]], minlength=N) > S2).any(): bad.append("splits of level 2")
    return bad
def reference(x, nb, bd):
    v, near, p, number, c1 = grow(x, nb, bd)
    O, S = np.nonzero(c1[:, :, 0] > T2)
    number2 = np.full(c1.shape[:2], -1); number2[O, S] = np.arange(len(O)); mid = c1[O, S]; val = {}; fine = {}
    for d in range(3):
        for b in range(2):
            m = near[p[S], 2 * d + b]; t = np.where((O >> d & 1) != b, S, number[m]); o = O ^ (1 << d)
            val[d, b] = np.where((t >= 0)[:, None], c1[o, t], v[m]); fine[d, b] = np.where(t >= 0, number2[o, t], -1)
    c2 = []
    for o in range(8):
        c = mid.copy()
        for d in range(3): c += 0.125 * (val[d, o >> d & 1] - mid)
        c2.append(c)
    c2 = np.stack(c2); z = 0.25 * c2
    for o in range(8):
        for d in range(3):
            b = o >> d & 1; other = c2[o ^ (1 << d)]; u = fine[d, b]
            z[o] += 0.125 * (other + np.where((u >= 0)[:, None], other[u], val[d, b]))
    y1 = np.zeros((N, 8, 16, S1)); y2 = np.zeros((N, 8, 16, S2))
    for r in range(N):
        a = c1[:, p // R == r]; y1[r, :, :, :a.shape[1]] = a.transpose(0, 2, 1)
        a = z[:, p[S] // R == r]; y2[r, :, :, :a.shape[1]] = a.transpose(0, 2, 1)
    return {"y1": y1.reshape(N, 128, S1).astype(np.float32), "y2": y2.reshape(N, 128, S2).astype(np.float32)}

import numpy as np
from concourse.bass import DstId, RemoteDMATransfer
from concourse.mybir import AluOpType, ActivationFunctionType

R, S1, S2, CAPP, N = 3072, 1024, 768, 16, 8
G0 = 16 + R
WO = G0 + 128
WG = WO + 2 * S1
NW = WG + 256
QG = 16 + S2
F, B, I, U = "float32", "bfloat16", "int32", "uint16"

SCRATCH = {"pcd": ("dram", [2, WO], B), "land3": ("sbuf", [128, 8, 96], B)}
for _d, _l in ((B, dict(win=NW + 16, pc=WO, xg=416, x0=24, mk=640, mb=27 * 128, bg=7 * 144, cob=216, e16b=16, rb=8, ub=136,
                        ur=16 * 136, mm=24 * 128, f1=24, c1=24, phl=48, gc=144, bx=128, s1=128, s2=256, s3=S2,
                        bq=256, ps=1056, f2=64, loc=64, rem=64, dif=128, nhl=128, gf=384, step=S2, sg=S2, msk=S2, n2=1168,
                        gp=S2, one=128, ut=S2, gn=S2, gg=4 * S2)),
               (F, dict(bdf=8, pay=384, sc=2432, io1=128, iom=128, iot=128, ioh=128, ior=128, hf=256, col=56, cell=24, kt=96, e16=16,
                        repf=128, big1=144, rc=24, bt=24, co=216, tm=256, mf=384, rd=384, urow=S2, w1=168, bn=128, wb=64,
                        y1s=S1, st=8, vf=64, ff=48 * 26, q=QG + 1024, hh=3 * S2, y2s=S2)),
               (I, dict(bdi=8, nbi=416, pi=16, vi=128, ii=192)),
               (U, dict(ob=8, operm=24, opos=24, o1=128, op=64, o2=16, oli=16, o3=48, olp=48, om=48, og=144, on=48, oq=144))):
    for _k in _l:
        SCRATCH[_k] = ("sbuf", [128, _l[_k]], _d)
for _k in "abcdefgh":
    SCRATCH["p" + _k + "_"] = ("psum", [128, 512], F)
SEMAPHORES = ["cv", "ca", "ct", "cg", "r1", "r2", "r3", "l1", "l2", "l3"] + ["d%d" % _k for _k in range(48)]
A = AluOpType
ACT = ActivationFunctionType
PLAN, TRIES, SEED = {}, 5000, 1
CASES, THRIFT, HEAT, LEAN = ((1.0, 1.0), (0.55, 1.0), (0.75, 1.4)), 2.0, 150.0, 300.0
CYC, PE, GAT, LAT = 1.04, 0.52, 1.55, 120.0


def emit(g, T, ops):
    Q = {"v": g.vector, "a": g.scalar, "t": g.tensor, "g": g, "s": g.sync}
    hist, pred = {}, []
    for n, op in enumerate(ops):
        pr = {}
        one = list(op["q"])[0] if len(op["q"]) == 1 else None
        for rs, isw in ((op["wr"], True), (op["rd"], False)):
            for (nm, p0, p1, c0, c1, st) in rs:
                psum = nm.endswith("_")
                for (w, m, a0, a1, b0, b1, bs) in hist.get(nm, ()):
                    same = one is not None and list(ops[m]["q"]) == [one]
                    if psum:
                        if same and one == "t":
                            pr[m] = pr.get(m, False)
                            continue
                        if same and not (w or isw):
                            continue
                    elif not (w or isw) or a1 <= p0 or p1 <= a0 or b1 <= c0 or c1 <= b0:
                        continue
                    elif st * bs > 1 and not set(range(c0, c1, st)) & set(range(b0, b1, bs)):
                        continue
                    pr[m] = True
        for m in op["after"]:
            pr[m] = pr.get(m, False)
        for m in list(pr):
            if any(pr[x] and pred[x].get(m) for x in pr if x != m):
                del pr[m]
        pred.append(pr)
        for rs, isw in ((op["wr"], True), (op["rd"], False)):
            for (nm, p0, p1, c0, c1, st) in rs:
                h = hist.setdefault(nm, [])
                if nm.endswith("_"):
                    h[:] = [e for e in h if not (list(ops[e[1]]["q"]) == list(op["q"]) == ["t"])]
                h.append((isw, n, p0, p1, c0, c1, st))
    n = len(ops)
    pl = [list(x.items()) for x in pred]
    sl = [[] for _ in range(n)]
    for k in range(n):
        for m, hard in pl[k]:
            sl[m].append((k, hard))
    cases = []
    for far, pe in CASES:
        cases.append(([{q: x[1] * (far if op["kind"] == "send" else pe if q == "t" else 1.0) for q, x in op["q"].items()} for op in ops],
                      [op["lat"] * (far if op["kind"] == "send" else 1.0) for op in ops]))

    def fit(order, back, cs, lat, lean):
        beg, end = {q: [] for q in Q}, {q: [] for q in Q}
        place = [None] * n
        for k in order:
            if back:
                t0 = lat[k]
                for m, hard in sl[k]:
                    x = place[m][1] + lat[k] if hard else place[m][1]
                    if x > t0:
                        t0 = x
            else:
                t0 = 0.0
                for m, hard in pl[k]:
                    x = place[m][1] + lat[m] if hard else place[m][1]
                    if x > t0:
                        t0 = x
            best = None
            for q, cost in cs[k].items():
                bq, eq = beg[q], end[q]
                lo, hi = 0, len(eq)
                while lo < hi:
                    mid = (lo + hi) >> 1
                    if eq[mid] > t0:
                        hi = mid
                    else:
                        lo = mid + 1
                t, last = t0, len(eq)
                while lo < last and t + cost > bq[lo]:
                    t = eq[lo]
                    lo += 1
                key = t + THRIFT * cost + (lean[k] if q == "v" else 0.0)
                if best is None or key < best[4]:
                    best = (t, t + cost, q, lo, key)
            place[k] = best
            beg[best[2]].insert(best[3], best[0])
            end[best[2]].insert(best[3], best[1])
        return place

    def length(place):
        order, total = sorted(range(n), key=lambda k: (place[k][0], k)), 0.0
        for cs, lat in cases:
            free, fin = {q: 0.0 for q in Q}, [0.0] * n
            for k in order:
                q = place[k][2]
                t = free[q]
                for m, hard in pl[k]:
                    x = fin[m] + lat[m] if hard else fin[m]
                    if x > t:
                        t = x
                fin[k] = free[q] = t + cs[k][q]
            total += max(fin[k] + lat[k] for k in range(n)) + 0.05 * sum(fin) / n
        return total / len(cases)
    if n not in PLAN:
        rng = np.random.default_rng(SEED)
        names = sorted({op["wr"][0][0][:3] for op in ops if op["wr"]})
        kin = np.array([names.index(op["wr"][0][0][:3]) if op["wr"] else -1 for op in ops])
        up = [0.0] * n
        for k in range(n - 1, -1, -1):
            up[k] += min(x[1] for x in ops[k]["q"].values())
            for m, hard in pl[k]:
                up[m] = max(up[m], up[k] + (ops[m]["lat"] if hard else 0.0))
        now, lean = 1e9, np.full(n, LEAN)
        for it in range(TRIES):
            cs, lat = cases[it % len(cases)]
            w = np.array(up) + rng.standard_normal(n) * (rng.random(n) < 0.3) * rng.choice([30.0, 100.0, 400.0])
            for _j in range(int(rng.integers(0, 4))):
                w[kin == rng.integers(0, len(names))] += rng.standard_normal() * 2500.0
            w = w.tolist()
            ln = np.where(rng.random(n) < 0.05, rng.choice([-500.0, 0.0, 500.0, 2000.0], n), lean).tolist()
            for k in range(n - 1, -1, -1):
                for m in pred[k]:
                    w[m] = max(w[m], w[k] + 1.0)
            place = fit(sorted(range(n), key=lambda k: (-w[k], k)), False, cs, lat, ln)
            bk = fit(sorted(range(n), key=lambda k: (-place[k][1], -k)), True, cs, lat, ln)
            place = fit(sorted(range(n), key=lambda k: (-bk[k][1], k)), False, cs, lat, ln)
            end = length(place)
            if n not in PLAN or end <= PLAN[n][0]:
                PLAN[n] = (end, place)
            if end <= now + HEAT * (1.0 - it / TRIES) * rng.exponential():
                now, up, lean = end, [x[1] for x in bk], np.array(ln)
    place = PLAN[n][1]
    cnt = {q: 0 for q in Q}
    seen = {q: {} for q in Q}
    tok, final, nd = [None] * n, {}, 0
    for k in sorted(range(n), key=lambda k: (place[k][0], k)):
        op, q = ops[k], place[k][2]
        need = {}
        for m, hard in pl[k]:
            if hard:
                need[tok[m][0]] = max(need.get(tok[m][0], 0), tok[m][1])
        for s in need:
            if seen[q].get(s, 0) < need[s]:
                Q[q].wait_ge(T.sem[s], need[s])
                seen[q][s] = need[s]
        ins = op["q"][q][0]()
        if op["kind"] == "dma":
            tok[k] = ("d%d" % nd, 16)
            nd += 1
            ins.then_inc(T.sem[tok[k][0]], 16)
        elif op["kind"] == "send":
            tok[k] = ("r%d" % op["round"], op["inc"])
            final["l%d" % op["round"]] = op["inc"]
        else:
            cnt[q] += 1
            tok[k] = ("c" + q, cnt[q])
            ins.then_inc(T.sem["c" + q], 1)
        final[tok[k][0]] = tok[k][1]
    for s in final:
        if max(seen[q].get(s, 0) for q in Q) < final[s]:
            g.wait_ge(T.sem[s], final[s])


def rank_program(g, core, T, topo):
    rank = T.rank_of(core)
    if rank is None:
        return
    ops = []

    def v(name, c0=0, c1=None, st=1, p0=0, p1=128):
        if c1 is None:
            c1 = SCRATCH[name][1][1]
        t = T[name]
        ap = t[p0:p1, c0:c1:st] if st > 1 else t[p0:p1, c0:c1]
        return (ap, [(name, p0, p1, c0, c1, st)], (c1 - c0 + st - 1) // st, SCRATCH[name][2], 0)

    def ind(w, o):
        return (w[0].indirect(o[0]), w[1] + o[1], 16 * o[2], w[3], 1)

    def regs(xs):
        return [r for x in xs if isinstance(x, tuple) for r in x[1]]

    def raw(x):
        return x[0] if isinstance(x, tuple) else x

    def run(q, wr, rd, lat=LAT, **k):
        ops.append(dict(q=q, wr=regs(wr), rd=regs(rd), lat=lat, kind=k.get("kind", "c"), after=k.get("after", ()),
                        round=k.get("round"), inc=k.get("inc")))

    def cost(i, xs, k=1.0):
        if i[4]:
            k = GAT
        elif k == 0.5 and any(x[3] not in (B, U) for x in xs if isinstance(x, tuple)):
            k = 1.0
        return max(64, i[2] * k) * CYC

    def ts(o, i, s1, op0, s2=None, op1=None):
        if op1 is None:
            fn = lambda: g.vector.tensor_scalar(o[0], i[0], raw(s1), None, op0)
        else:
            fn = lambda: g.vector.tensor_scalar(o[0], i[0], raw(s1), raw(s2), op0, op1)
        alt = {"v": (fn, cost(i, [o, i, s1, s2], 0.5))}
        cols = [x for x in (s1, s2) if isinstance(x, tuple)]
        if o[3] in (F, B) and i[3] in (F, B) and all(x[3] == F and not x[1][0][0].endswith("_") for x in cols):
            kw = None
            if op0 == A.mult and op1 is None:
                kw = dict(scale=raw(s1))
            elif op0 == A.add and op1 is None:
                kw = dict(bias=raw(s1))
            elif op0 == A.mult and op1 == A.add:
                kw = dict(scale=raw(s1), bias=raw(s2))
            if kw:
                alt["a"] = (lambda: g.scalar.activation(o[0], i[0], ACT.Identity, **kw), cost(i, []) + 15)
        run(alt, [o], [i, s1, s2])

    def tt(o, a, b, op):
        two = 1.0 if (a[1][0][0].endswith("_") or b[1][0][0].endswith("_")) else 2.0
        run({"v": (lambda: g.vector.tensor_tensor(o[0], a[0], b[0], op), cost(a, [], two))}, [o], [a, b])

    def cp(o, i, q="va"):
        alt = {"v": (lambda: g.vector.tensor_copy(o[0], i[0]), cost(i, [o, i], 0.5))}
        if "a" in q and o[3] in (F, B) and i[3] in (F, B):
            alt["a"] = (lambda: g.scalar.activation(o[0], i[0], ACT.Copy), cost(i, []) + 15)
        run(alt, [o], [i])

    def sca(o, i, s, sb):
        run({"a": (lambda: g.scalar.activation(o[0], i[0], ACT.Identity, scale=s[0]), cost(i, []) + 15),
             "v": (lambda: g.vector.tensor_scalar(o[0], i[0], sb[0], None, A.mult), cost(i, [], 0.5))}, [o], [i, s, sb])

    def ms(o, c, free=True):
        alt, rd = {"v": (lambda: g.vector.memset(o[0], c), cost(o, [o], 0.5))}, []
        if free and o[2] <= 128:
            z = v("io1", 0, o[2], p0=o[1][0][1], p1=o[1][0][2])
            alt["a"], rd = (lambda: g.scalar.activation(o[0], z[0], ACT.Identity, scale=0.0, bias=c), cost(o, []) + 15), [z]
        run(alt, [o], rd)

    def fill(o, z):
        run({"v": (lambda: g.vector.memset(o[0], 0.0), cost(o, [o], 0.5)),
             "a": (lambda: g.scalar.activation(o[0], z[0], ACT.Copy), cost(z, []) + 15)}, [o], [z])

    def scan(o, a):
        run({"v": (lambda: g.vector.tensor_tensor_scan(o[0], a[0], a[0], 0.0, A.add, A.max), 70.0)}, [o], [a])

    def mm(o, l, r, start=True, stop=True):
        run({"t": (lambda: g.tensor.matmul(o[0], l[0], r[0], start, stop), max(64, r[2]) * PE * (4 if l[3] == F else 1))}, [o], [l, r], LAT + 50)

    def iota(o, pat, base=0, cm=0):
        if o[3] != I:
            fn = lambda: g.iota(o[0], pat, base, cm, allow_small_or_imprecise_dtypes=True)
        else:
            fn = lambda: g.iota(o[0], pat, base, cm)
        run({"g": (fn, (2 * o[2] + 130) * CYC)}, [o], [])

    def dma(o, i, lat=2200.0, q="sa", after=()):
        alt = {"s": (lambda: g.sync.dma_start(raw(o), raw(i)), 70.0)}
        if "a" in q:
            alt["a"] = (lambda: g.scalar.dma_start(raw(o), raw(i)), 90.0)
        run(alt, [o], [i], lat, kind="dma", after=after)

    peers = [q for q in range(N) if q != rank]
    far = [q for q in peers if topo.chip(T.cores[q]) != topo.chip(core)]
    used, engs = [], {}
    for q in far + [q for q in peers if q not in far]:
        e = [k for k in topo.engines(core, T.cores[q]) if k not in used][:2]
        used += e
        engs[q] = (1 << e[0]) | (1 << e[1])

    def send(k, src, dst, land, issue, lat):
        def fn():
            trs = []
            for q in peers:
                rid, pid, _se = topo.addr(T.cores[q])
                trs.append(RemoteDMATransfer(dst_ids=[DstId(rid=rid, pnc=pid)], dma_engine_mask=engs[q],
                                             remote_sem=T.sem["r%d" % k], src=src(q)[0], dst=dst))
            return g.remote_dma_fused(trs, local_sem=T.sem["l%d" % k])
        run({"g": (fn, issue)}, [land(q) for q in peers], [src(q) for q in peers], lat, kind="send", round=k, inc=2 * len(peers))

    def wrap(out, slot, src, n, w=16):
        stp = 16 // w
        for r in range(w):
            a = slot * 144 + 16 - stp - stp * r
            mm(out, v("bg", a, a + 128), v(src, r, w * n, w), r == 0, r == w - 1)

    def spread(pk, src, n):
        for d in range(3):
            mm(v(pk, n * d, n * d + n), v("rd", 128 * d, 128 * d + 128), src)

    def c(k):
        return v("col", k, k + 1)
    P, RR, GG, ROLE, H, AND0, ROLE2 = 0, 1, 2, 3, 4, 5, 8
    RH, LAM, CB, CORR, PW, CH, PL, NR, LS, LH, XO, HI, LOW, SR = 9, 13, 14, 15, 16, 17, 20, 24, 28, 29, 30, 33, 34, 35
    T0, T1, T2, T3, T4, T5, T6, T7, HX = 38, 39, 40, 41, 42, 43, 44, 45, 46
    TRI, SH, IDB, REPB, THM = 0, 128, 256, 384, 512

    iota(v("nbi", 16, 400), [[1, 384]], 0, 24)
    dma(v("x0"), T.x[0:1, :])
    dma(v("bdi", p1=16), T.bd[:, :])
    for k in range(8):
        dma(v("xg", 16, 400, p0=16 * k, p1=16 * k + 16), T.x[:, 384 * k:384 * k + 384], 2400.0)
    iota(v("pi", 0, 1), [[0, 1]], 0, 1)
    iota(v("io1"), [[1, 128]])
    iota(v("iom"), [[0, 8], [1, 16]])
    iota(v("cell"), [[1, 24]], 0, 24)
    iota(v("rc", 0, 8), [[1, 2], [2, 4]])
    iota(v("rc", 8, 16), [[-1, 2], [2, 4]], 1)
    iota(v("rc", 16, 24), [[0, 2], [2, 4]])
    iota(v("ioh", p1=16), [[0, 8], [1, 8], [0, 2]])
    for d in range(6):
        dma((T.nbi[d:128:16, 16:400], [("nbi", d, d + 1, 16, 400, 1)]), T.nb[d:d + 1, :], 2400.0, "s")
    for k in range(8):
        dma(v("win", 16, G0, p0=16 * k, p1=16 * k + 16), T.x[:, :], 2600.0 + 450 * k, "s", range(len(ops) - 6 - k, len(ops)))
    ms(v("y2s", 0, 402), 0.0)
    for k in range(4):
        fill(v("sc", 256 * k, 256 * k + 256), v("y2s", 0, 256))
    ms(v("xg", 0, 16), 0.0, False)
    ms(v("xg", 400, 416), 0.0, False)
    ms(v("big1"), 0.0)
    for k in range(8):
        fill(v("pc", 402 * k, 402 * k + 402), v("y2s", 0, 402))
    p_ = v("pi", 0, 1)
    ts(v("pi", RR, RR + 1), p_, 15, A.bitwise_and)
    ts(v("pi", GG, GG + 1), p_, 4, A.arith_shift_right)
    ts(v("pi", ROLE, ROLE + 1), p_, 4, A.arith_shift_right, 3, A.bitwise_and)
    ts(v("pi", H, H + 1), p_, 6, A.arith_shift_right)
    for d in range(3):
        ts(v("pi", AND0 + d, AND0 + d + 1), p_, 4, A.arith_shift_right, 1 << d, A.bitwise_and)
    ts(v("pi", ROLE2, ROLE2 + 1), p_, 3, A.arith_shift_right, 6, A.bitwise_and)
    cp(v("col", 0, 3), v("pi", 0, 3))
    cp(v("col", 3, 9), v("pi", 3, 9))
    ts(v("repf", p1=16), v("iom", p1=16), v("col", RR, RR + 1, p1=16), A.is_equal)
    ts(c(CB), c(GG), -384.0, A.mult, 16.0, A.add)
    ts(c(T0), c(RR), 6.0, A.is_ge, -24.0, A.mult)
    ts(v("mk", TRI, TRI + 128), v("io1"), c(P), A.is_gt)
    ts(v("mk", REPB, REPB + 128), v("iom"), c(RR), A.is_equal)
    ts(v("kt", 0, 24), v("cell"), c(CB), A.add, 1008.0, A.add)
    ts(v("kt", 24, 48), v("cell"), c(CB), A.add, 1009.0, A.add)
    ts(v("operm"), v("cell"), c(CB), A.add)
    ts(c(CORR), c(T0), c(RR), A.mult, 16.0, A.add)
    ts(v("nbi", 0, 16), v("io1", 0, 16), 0.0, A.mult, c(CORR), A.subtract)
    ts(v("nbi", 400, 416), v("io1", 0, 16), 0.0, A.mult, c(CORR), A.subtract)
    for s in range(2):
        ts(v("big1", 14 + s, 128 + 14, 16), v("rc", 8 * s, 8 * s + 8), c(RR), A.is_equal)
        ts(v("hf", 128 * s, 128 * s + 128, p1=16), v("ioh", p1=16), 8.0 * s, A.add, v("col", RR, RR + 1, p1=16), A.is_equal)
    for k in range(3):
        fill(v("bg", 336 * k, 336 * k + 336), v("y2s", 0, 336))
    ts(v("e16"), v("io1", 0, 16), c(RR), A.is_equal)
    z8 = v("io1", 0, 8)
    for s in range(2):
        ts(v("bg", 5 * 144 + 14 + s, 5 * 144 + 142, 16), z8, 0.0, A.mult, v("e16", 0, 1), A.add)

    cp(v("bdf", p1=16), v("bdi", p1=16))
    mm(v("pa_", 0, 8), v("repf", p1=16), v("bdf", p1=16))
    ts(v("ob"), v("pa_", 0, 8), c(CB), A.add, 400.0, A.min)
    cp(v("bx"), ind(v("xg"), v("ob")))
    mm(v("pa_", 0, 128), v("mk", REPB, REPB + 128), v("bx"))
    cp(v("s1"), v("pa_", 0, 128))
    send(1, lambda q: v("s1", 16 * q, 16 * q + 16), T.win[:, G0 + 16 * rank:G0 + 16 * rank + 16],
         lambda q: v("win", G0 + 16 * q, G0 + 16 * q + 16), 2500.0, 4000.0)
    ts(v("f1"), v("x0"), 0.0, A.is_gt)
    scan(v("c1"), v("f1"))
    mm(v("pb_", 0, 1), v("mk", TRI, TRI + 128), v("c1", 23, 24))
    tt(v("w1", 0, 24), v("c1"), v("kt", 24, 48), A.subtract)
    tt(v("w1", 24, 48), v("w1", 0, 24), v("f1"), A.mult)
    tt(v("w1", 48, 72), v("w1", 24, 48), v("kt", 0, 24), A.add)
    ts(v("opos"), v("w1", 48, 72), v("pb_", 0, 1), A.add)
    ts(v("w1", 72, 96), v("c1"), v("pb_", 0, 1), A.add, 2.0, A.mult)
    ts(v("pay"), ind(v("nbi"), v("operm")), c(CORR), A.add)
    ts(v("kt", 48, 72), v("cell"), -1.0, A.mult, float(WO - 18), A.add)
    ts(v("kt", 72, 96), v("cell"), 16.0, A.add)
    tt(v("w1", 96, 120), v("w1", 72, 96), v("kt", 48, 72), A.add)
    tt(v("w1", 120, 144), v("w1", 96, 120), v("f1"), A.mult)
    tt(v("w1", 144, 168), v("w1", 120, 144), v("kt", 72, 96), A.add)
    cp(v("phl", 0, 24), v("w1", 144, 168), "v")
    tt(v("phl", 24, 48), v("w1", 144, 168), v("phl", 0, 24), A.subtract)
    run({"v": (lambda: g.vector.tensor_copy(T.sc[:, :].indirect(T.opos[:, :]), T.pay[:, :]), 1500.0)}, [v("sc")], [v("opos"), v("pay")])
    dma(v("pcd", 16, G0, p0=0, p1=1), v("phl", 0, 24), q="s")
    dma(v("pcd", 16, G0, p0=1, p1=2), v("phl", 24, 48), q="s")
    iota(v("gc", 16, 144, p1=2), [[2, 128]], 16)
    ms(v("gc", 0, 16, p1=2), 0.0)
    ms(v("gc", 16, 144, p1=1), float(WG - 16))
    dma(v("pcd", 0, 16, p1=2), v("gc", 0, 16, p1=2), q="s")
    dma(v("pcd", G0, WO, p1=2), v("gc", 16, 144, p1=2), q="s")
    for k in (0, 4, 1, 5, 2, 6):
        dma(v("pc", p0=16 * k, p1=16 * k + 2), v("pcd", p1=2), q="s")
    ts(v("bn"), ind(v("nbi"), v("ob")), c(CORR), A.add)
    for r in range(8):
        mm(v("pc_", 0, 16), v("big1", 14 - 2 * r, 142 - 2 * r), v("bn", r, 128, 8), r == 0, r == 7)
    for s in range(2):
        mm(v("pd_", s, 16, 2), v("hf", 128 * s, 128 * s + 128, p1=16), v("bdf", p1=16))
    wrap(v("pd_", 16, 32), 5, "bx", 16, 8)
    ts(v("wb", 0, 16), v("pd_", 0, 16), 16.0, A.add)
    ts(v("wb", 16, 32), v("pd_", 16, 32), 0.0, A.is_gt)
    tt(v("wb", 32, 48), v("pc_", 0, 16), v("wb", 0, 16), A.subtract)
    cp(v("oli"), v("pc_", 0, 16))
    tt(v("wb", 48, 64), v("wb", 32, 48), v("wb", 16, 32), A.mult)
    tt(v("wb", 32, 48), v("wb", 48, 64), v("wb", 0, 16), A.add)
    cp(v("o2"), v("wb", 32, 48))
    for k, pk in enumerate(("pb_", "pg_")):
        for r in range(8):
            mm(v(pk, 0, 64), v("big1", 14 - 2 * r, 142 - 2 * r), v("sc", 512 * k + r, 512 * k + 512, 8), r == 0, r == 7)
        cp(v("o1", 64 * k, 64 * k + 64), v(pk, 0, 64))
        cp(v("op", p0=64 * k, p1=64 * k + 64), v("o1", 64 * k, 64 * k + 64, p0=64 * k, p1=64 * k + 64))

    iota(v("bt", 0, 8), [[0, 4], [1, 2]])
    iota(v("bt", 8, 16), [[0, 2], [1, 2], [0, 2]])
    iota(v("bt", 16, 24), [[1, 2], [0, 4]])
    iota(v("iot"), [[0, 16], [16, 8]])
    for k in range(3):
        iota(v("urow", 256 * k, 256 * k + 256), [[1, 256]], 256 * k)
        iota(v("ut", 256 * k, 256 * k + 256, p1=2), [[0, 16], [1, 16]])
        iota(v("ut", 256 * k, 256 * k + 256, p1=1), [[16, 16], [0, 16]], 256 * k)
    ms(v("win", 0, 16), 0.0)
    ms(v("win", NW, NW + 16), 0.0)
    ms(v("n2", 1153, 1154), 0.0)
    ms(v("win", G0 + 16 * rank, G0 + 16 * rank + 16), 0.0)
    ms(v("win", WG + 32 * rank, WG + 32 * rank + 32), 0.0)
    ms(v("co"), 0.0)
    ts(v("col", RH, RH + 4), v("io1", 0, 4), c(ROLE), A.is_equal)
    ts(v("col", HX, HX + 4), v("col", RH, RH + 4), c(H), A.not_equal)
    ts(c(LOW), c(RR), 2.0, A.is_lt)
    ts(c(LAM), c(RH + 3), 0.5, A.mult, 0.125, A.add)
    for d in range(3):
        ts(v("tm", 8 * d, 8 * d + 8), v("bt", 8 * d, 8 * d + 8), c(RH + d), A.mult)
    tt(v("tm", 24, 32), v("tm", 0, 8), v("tm", 8, 16), A.add)
    ts(v("col", NR, NR + 4), v("col", RH, RH + 4), -2.0, A.mult, 1.0, A.add)
    tt(v("tm", 32, 40), v("tm", 24, 32), v("tm", 16, 24), A.add)
    ms(v("co", 3, 48, 4), 1.0 / 128)
    ts(v("tm", 168, 176), v("tm", 32, 40), c(H), A.is_equal, c(LAM), A.mult)
    for d in range(3):
        for b in range(2):
            a = (2 * d + b) * 8 + d
            ms(v("co", a, a + 5, 4), (2 * b - 1) / 128)
    ts(v("bg", 15, 143, 16), v("tm", 168, 176), v("e16", 0, 1), A.mult)
    ts(c(T1), c(H), 2.0, A.mult, -1.0, A.add)
    ts(c(T2), c(H), -1.0, A.mult, 1.0, A.add)
    cp(v("rb"), v("tm", 168, 176))
    cp(v("co", 48, 56), v("tm", 168, 176))
    ts(v("tm", 40, 64), v("bt"), c(H), A.is_equal)
    ts(c(LS), c(T1), c(LAM), A.mult, 1.0 / 128, A.mult)
    ts(c(LH), c(T2), c(LAM), A.mult)
    ts(c(T3), c(LAM), 1.0 / 128, A.mult)
    ts(c(SR), c(NR + 3), -1.0, A.mult)
    ts(v("tm", 64, 88), v("tm", 40, 64), 11.0 / 64, A.mult, 1.0 / 64, A.add)
    ts(v("co", 67, 88, 4), v("io1", 0, 6), 0.0, A.mult, c(T3), A.add)
    for d in range(3):
        ts(v("co", 64 + 9 * d, 64 + 9 * d + 5, 4), v("io1", 0, 2), 0.0, A.mult, c(LS), A.add)
    ts(c(T4), c(LH), -6.0 / 128, A.mult)
    ts(c(T5), c(LH), 25.0 / 64, A.mult)
    ts(v("co", 96, 120), v("tm", 64, 88), c(LAM), A.mult)
    ts(v("tm", 88, 96), v("tm", 32, 40), 2.0, A.mult, c(SR), A.add)
    ts(v("co", 91, 96, 4), v("io1", 0, 2), 0.0, A.mult, c(T4), A.add)
    ts(v("co", 120, 128), z8, 0.0, A.mult, c(T5), A.add)
    for d in range(3):
        ts(v("tm", 96 + 8 * d, 104 + 8 * d), v("tm", 40 + 8 * d, 48 + 8 * d), c(NR + d), A.mult)
        tt(v("co", 128 + 8 * d, 136 + 8 * d), v("tm", 96 + 8 * d, 104 + 8 * d), v("tm", 88, 96), A.mult)
    ts(v("tm", 200, 224), v("bt"), -2.0 / 128, A.mult, 1.0 / 128, A.add)
    for d in range(3):
        ts(v("tm", 176 + 8 * d, 184 + 8 * d), v("tm", 32, 40), c(HX + d), A.is_equal, c(LAM), A.mult)
        for hh in range(2):
            tt(v("co", 152 + 4 * hh + d, 216, 8), v("tm", 176 + 8 * d, 184 + 8 * d), v("tm", 200 + 8 * d, 208 + 8 * d), A.mult)
    tt(v("tm", 224, 232), v("tm", 176, 184), v("tm", 184, 192), A.add)
    ts(v("tm", 232, 240), v("tm", 168, 176), -6.0, A.mult)
    tt(v("tm", 240, 248), v("tm", 224, 232), v("tm", 192, 200), A.add)
    tt(v("tm", 248, 256), v("tm", 240, 248), v("tm", 232, 240), A.add)
    for hh in range(2):
        ts(v("co", 155 + 4 * hh, 216, 8), v("tm", 248, 256), 1.0 / 128, A.mult)
    cp(v("cob"), v("co"))
    cp(v("e16b"), v("e16"))
    for k in range(16):
        sca((v("mb", k, 27 * 128, 16)[0], [("mb%d" % k, 0, 128, 0, 1, 1)], 216, B, 0), v("cob"), v("e16", k, k + 1), v("e16b", k, k + 1))

    def mb(k, n=1):
        x = v("mb", 128 * k, 128 * (k + n))
        return (x[0], [("mb%d" % j, 0, 128, 0, 1, 1) for j in range(16)], x[2], B, 0)
    ms(v("bg", 144 + 15, 144 + 143, 16), 0.5)
    ms(v("bg", 144 + 15, 144 + 143, 16, p0=64), 0.0)
    ms(v("dif", 64, 128), 0.0)
    ms(v("bg", 288 + 15, 288 + 143, 16), 64.0)
    iota(v("ior"), [[16, 2], [0, 4], [1, 16]])
    ts(c(PL), c(H), 16.0, A.mult, c(RR), A.add)
    for d in range(3):
        ts(v("rd", 128 * d, 128 * d + 128), v("ior"), c(PL), A.is_equal, c(RH + d), A.mult)
    ts(v("bg", 3 * 144 + 15, 3 * 144 + 143, 16), v("rc", 16, 24), c(ROLE2), A.is_equal, c(LOW), A.mult)
    ts(v("bg", 6 * 144 + 15, 6 * 144 + 143, 16), v("bg", 3 * 144 + 15, 3 * 144 + 143, 16), c(T2), A.mult)
    ts(v("bg", 4 * 144 + 15, 4 * 144 + 143, 16), z8, c(GG), A.is_equal)
    ts(v("mk", IDB, IDB + 128), v("io1"), c(P), A.is_equal)
    ts(v("mk", SH, SH + 128), v("io1"), -1.0, A.add, c(P), A.is_equal)
    ts(v("mk", THM, THM + 128), v("iot"), c(P), A.is_gt)
    ms(v("one", p1=2), 1.0)
    ms(v("ps", 0, 16), 0.0)
    ms(v("ps", 1040, 1056), 0.0)
    ts(c(CH), c(H), -1024.0, A.mult, 16.0, A.add)
    ts(c(T6), c(ROLE), -2.0, A.mult, 4.0, A.add)
    ts(c(T7), c(ROLE), -1.0, A.mult, 3.0, A.add)
    ts(c(HI), c(GG), 128.0, A.mult, float(QG), A.add)
    ts(c(PW), c(T6), c(T7), A.max)
    ms(v("ub"), 0.0)
    ms(v("tm", 120, 160), 0.0)
    for d in range(3):
        ts(c(XO + d), c(AND0 + d), -2.0, A.mult, c(GG), A.add)
        ts(v("tm", 121 + 12 * d, 129 + 12 * d), z8, float(-(1 << d)), A.add, c(XO + d), A.is_equal)
        tt(v("ub", 8 + 16 * d, 16 + 16 * d), v("tm", 121 + 12 * d, 129 + 12 * d), v("tm", 120 + 12 * d, 128 + 12 * d), A.subtract)
    cp(v("ub", 72, 136), v("ub", 8, 72))
    for r in range(16):
        sca(v("ur", 136 * r, 136 * r + 136), v("ub"), v("e16", r, r + 1), v("e16b", r, r + 1))
    for o in range(8):
        for d in range(3):
            oo = o ^ (1 << d)
            sca(v("mm", (3 * o + d) * 128, (3 * o + d) * 128 + 128), mb(2 * d + (o >> d & 1)), v("tm", 168 + oo, 169 + oo), v("rb", oo, oo + 1))
    cp(v("mf"), mb(16, 3))
    ms(v("q", 0, 16), 0.0)
    ms(v("n2", 0, 1), 0.0)
    ms((T.land3[:, rank, :], [("land3", 0, 128, rank, rank + 1, 1)], 96, B, 0), 0.0, False)

    roots = v("win", 0, WO)
    cp(v("s2"), ind(roots, v("o2")))
    send(2, lambda q: v("s2", 32 * q, 32 * q + 32), T.win[:, WG + 32 * rank:WG + 32 * rank + 32],
         lambda q: v("win", WG + 32 * q, WG + 32 * q + 32), 1000.0, 4200.0)
    for k in range(4):
        cp(v("win", WO + 512 * k, WO + 512 * k + 512), ind(roots, v("o1", 32 * k, 32 * k + 32)))
    for k in range(2):
        mm(v("pe_" if k == 0 else "pf_", 0, 384), v("one", p1=2), v("ut", 384 * k, 384 * k + 384, p1=2), True, False)
    for r in range(16):
        mm(v("pa_", 0, 64), v("bg", 15 - r, 143 - r), v("win", WO + 128 * r, WO + 128 * r + 128, 2), r == 0, r == 15)
    ts(v("f2"), v("pa_", 0, 64), 100.0, A.is_gt)
    scan(v("loc"), v("f2"))
    ts(v("rem"), v("loc"), -1.0, A.mult, v("loc", 63, 64), A.add)
    mm(v("pa_", 128, 129), v("mk", TRI, TRI + 128), v("loc", 63, 64))
    mm(v("pa_", 129, 130), v("mk", THM, THM + 128), v("loc", 63, 64))
    cp(v("st", 0, 2), v("pa_", 128, 130), "v")
    mm(v("pb_", 64, 128), v("mk", IDB, IDB + 128), v("loc"), True, False)
    mm(v("pb_", 64, 128), v("mk", SH, SH + 128), v("rem"), False, True)
    ts(v("dif", 0, 64), v("pb_", 64, 128), -1.0, A.mult)
    for k in range(2):
        cp(v("ps", 16 + 512 * k, 528 + 512 * k), ind(v("pc"), v("op", 32 * k, 32 * k + 32)))
    cp(v("bq"), ind(v("pc"), v("oli")))
    wrap(v("pd_", 0, 16), 6, "bq", 16)
    cp(v("wb", 0, 16), v("pd_", 0, 16))
    spread("pd_", v("wb", 0, 16), 16)
    for k in range(6):
        cp(v("o3", k, 48, 6), v("pd_", 16 * (k // 2) + k % 2, 16 + 16 * (k // 2), 2), "v")
    full = v("win")
    for k in range(2):
        cp(v("s3", 384 * k, 384 * k + 384), ind(full, v("o3", 24 * k, 24 * k + 24)))
    send(3, lambda q: v("s3", 96 * q, 96 * q + 96), T.land3[:, rank, :], lambda q: (None, [("land3", 0, 128, q, q + 1, 1)]), 1000.0, 7000.0)

    def sign(k):
        o_, i_ = v("sg", 384 * k, 384 * k + 384), v("pe_" if k == 0 else "pf_", 0, 384)
        ts(v("step", 384 * k, 384 * k + 384), v("urow", 384 * k, 384 * k + 384), v("st", 0, 1), A.is_ge)
        mm(i_, v("dif"), v("step", 384 * k, 384 * k + 384), False, True)
        run({"a": (lambda: g.scalar.activation(o_[0], i_[0], ACT.Sign, bias=0.5), 415.0)}, [o_], [i_])
    sign(0)
    sign(1)
    for r in range(16):
        mm(v("pa_", 0, 48), v("bg", 288 + 15 - r, 288 + 143 - r), v("step", r, S2, 16), r == 0, False)
    for r in range(16):
        mm(v("pa_", 0, 48), v("bg", 144 + 15 - r, 144 + 143 - r), v("sg", r, S2, 16), False, r == 15)
    for k in range(2):
        mm(v("pc_" if k == 0 else "pd_"), mb(6), v("win", WO + 1024 * k, WO + 1024 * k + 1024, 2))
        y_ = v("y1s", 512 * k, 512 * k + 512)
        cp(y_, v("pc_" if k == 0 else "pd_"))
        dma(T.y1[:, 512 * k:512 * k + 512], (y_[0], y_[1] + [("land3", 0, 128, 0, 8, 1)]), 4000.0, "s")
    ts(v("vf"), v("loc"), v("st", 0, 1), A.add, 15.0, A.add)
    tt(v("vi", 0, 64), v("vf"), v("f2"), A.mult)
    ts(v("vi", 64, 128), v("vi", 0, 64), 2032, A.bitwise_and)
    cp(v("nhl", 0, 64), v("vi", 64, 128))
    tt(v("nhl", 64, 128), v("vi", 0, 64), v("vi", 64, 128), A.subtract)

    ix, yi, ee, orl = v("ii", 0, 48), v("ii", 48, 96), v("ii", 96, 144), v("ii", 144, 192)
    BIG = float(1 << 24)

    def f(k, n=1):
        return v("ff", 48 * k, 48 * (k + n))
    ts(ix, v("pa_", 0, 48), -32.0, A.add)
    ts(yi, v("pa_", 0, 48), -32.0, A.add, c(PW), A.mult)
    ts(ee, ix, 8192 + 1023, A.bitwise_and)
    ts(orl, yi, 12, A.arith_shift_right, 1, A.bitwise_and)
    ts(f(0), ee, 2.0, A.mult, c(CH), A.add)
    ts(f(2), orl, c(H), A.not_equal)
    tt(f(1), f(0), f(2), A.add)
    ts(v("olp"), f(1), 1040.0, A.min)
    for k in range(2):
        cp(v("gp", 384 * k, 384 * k + 384), ind(v("ps"), v("olp", 24 * k, 24 * k + 24)))
    ts(f(4), ee, 2.0, A.mult, float(WO), A.add)
    tt(f(5), f(4), f(2), A.add)
    ts(v("om"), f(5), float(NW), A.min)
    for d in range(3):
        ts(f(6 + d), f(2), c(NR + d), A.mult, c(RH + d), A.add)
    ts(f(9), f(2), BIG, A.mult)
    ts(f(10), f(2), -BIG, A.mult, BIG, A.add)
    tt(f(11), f(10), f(4), A.max)
    wrap(v("pa_", 0, 48), 3, "gp", 48)
    tt(f(12), v("pa_", 0, 48), f(9), A.add)
    tt(f(13), f(12), f(11), A.min)
    spread("pg_", f(13), 48)
    ts(f(14), f(13), 0.5, A.mult, 1.0 - 0.5 * WO, A.add)
    ts(v("on"), f(14), 1153.0, A.min)
    ts(f(15, 3), v("pg_", 0, 144), float(WO), A.is_ge)
    tt(f(18, 3), f(15, 3), f(6, 3), A.mult)
    tt(f(21, 3), v("pg_", 0, 144), f(18, 3), A.add)
    ts(v("og"), f(21, 3), float(NW), A.min)
    for k in range(2):
        cp(v("gg", 3 * S2 + 384 * k, 3 * S2 + 384 * k + 384), ind(full, v("om", 24 * k, 24 * k + 24)))
        for j in range(3):
            cp(v("gg", j * S2 + 384 * k, j * S2 + 384 * k + 384), ind(full, v("og", 48 * j + 24 * k, 48 * j + 24 * k + 24)))
    for r in range(16):
        for s in range(2):
            mm(v("pe_" if r < 8 else "pf_", 64 * (r % 8), 64 * (r % 8) + 64), v("ur", 136 * r + 8 - 8 * s, 136 * r + 136 - 8 * s),
               v("nhl", 64 * s, 64 * s + 64), s == 0, s == 1)
        if r % 8 == 7:
            cp(v("n2", 1 + 64 * (r - 7), 65 + 64 * r), v("pe_" if r < 8 else "pf_"))
    mm(v("pb_", 0, 128), v("bg", 15, 143), v("win", WG, NW, 2))
    ts(v("gf", 0, 128), v("pb_", 0, 128), 100.0, A.is_gt, c(HI), A.mult)
    ts(v("gf", 128, 256), v("pb_", 0, 128), 100.0, A.is_gt)
    tt(v("gf", 256, 384), v("gf", 128, 256), v("io1"), A.mult)
    mm(v("pb_", 128, 256), v("ur", 8, 136), v("gf", 0, 128), True, False)
    mm(v("pb_", 128, 256), v("ur", 0, 128), v("gf", 256, 384), False, True)
    cp(v("n2", 1025, 1153), v("pb_", 128, 256))
    for k in range(2):
        ts(v("msk", 384 * k, 384 * k + 384), v("urow", 384 * k, 384 * k + 384), v("st", 1, 2), A.is_ge)
        tt(v("gn", 384 * k, 384 * k + 384), ind(v("n2", 0, 1154), v("on", 24 * k, 24 * k + 24)), v("msk", 384 * k, 384 * k + 384), A.mult)

    for k in range(2):
        for j in (3, 0, 1, 2):
            mm(v("pc_" if k == 0 else "pd_", 0, 384), mb(8 + j), v("gg", j * S2 + 384 * k, j * S2 + 384 * k + 384), j == 3, j == 2)
        cp(v("q", 16 + 384 * k, 400 + 384 * k), v("pc_" if k == 0 else "pd_", 0, 384))
    wrap(v("pa_", 0, 48), 4, "gn", 48)
    cp(f(24), v("pa_", 0, 48))
    spread("pb_", f(24), 48)
    cp(v("oq"), v("pb_", 0, 144))
    for o in range(8):
        pk, a0 = "pe_" if o % 4 < 2 else "pf_", 256 * (o // 4)
        out = v(pk, a0 + 128 * (o % 2), a0 + 128 * (o % 2) + 128)
        mm(out, mb(19 + o), v("win", WG, NW, 2), True, False)
        for d in range(3):
            a = 32 * d + (o >> d & 1)
            mm(out, v("mm", (3 * o + d) * 128, (3 * o + d) * 128 + 128),
               (T.land3[:, :, a:32 * d + 32:2], [("land3", 0, 128, 0, 8, 1)], 128, B, 0), False, d == 2)
        if o % 2:
            cp(v("q", QG + 128 * (o - 1), QG + 128 * (o + 1)), v(pk, a0, a0 + 256))

    for k, (pk, a, b) in enumerate((("pg_", 0, 320), ("ph_", 320, 576), ("pa_", 576, S2))):
        for j in (3, 0, 1, 2):
            mm(v(pk, 0, b - a), mb(12 + j), v("gg", j * S2 + a, j * S2 + b), j == 3, False)
        for d in range(3):
            cp(v("hh", d * S2 + a, d * S2 + b), ind(v("q"), v("oq", 48 * d + a // 16, 48 * d + b // 16)))
            mm(v(pk, 0, b - a), v("mf", 128 * d, 128 * d + 128), v("hh", d * S2 + a, d * S2 + b), False, d == 2)
        cp(v("y2s", a, b), v(pk, 0, b - a))
        dma(T.y2[:, a:b], v("y2s", a, b), 4200.0 - 750 * k, "s")
    emit(g, T, ops)
